import numpy as np
import ml_dtypes


def mxq(x, axis, fmt="e4m3"):
    dtype, down = {"e4m3": (ml_dtypes.float8_e4m3fn, 7), "e5m2": (ml_dtypes.float8_e5m2, 14)}[fmt]
    v = np.moveaxis(np.asarray(x, np.float32).astype(ml_dtypes.bfloat16).astype(np.float64), axis, -1)
    blocks = v.reshape(v.shape[:-1] + (-1, 32))
    amax = np.abs(blocks).max(-1, keepdims=True)
    byte = np.maximum(np.where(amax > 0, np.frexp(amax)[1] - 1 + 127, 0) - down, 1)
    scale = np.exp2(byte - 127.0)
    codes = (blocks / scale).astype(np.float32).astype(dtype).astype(np.float64)
    return np.moveaxis((codes * scale).reshape(v.shape), -1, axis)


WIDE = False


def mx_kscale(k):
    if not WIDE:
        return np.ones(k)
    levels = np.array([10, -10, 5, -5, 0])
    if k % 512:
        return np.exp2(np.random.permutation(np.resize(levels, k // 32))).repeat(32)
    a = np.empty((k // 512, 16))
    for p in range(k // 512):
        a[p, :8] = np.random.permutation(np.resize(levels, 8))
        for g in range(8):
            far = levels[np.abs(levels - a[p, g]) >= 10]
            a[p, g + 8] = far[np.random.randint(len(far))]
    return np.exp2(a.ravel()).repeat(32)


def f64(x):
    return np.asarray(x).astype(np.float64)


def striped(idx):
    return np.tile(np.asarray(idx).reshape(-1, 16).T, (8, 1)).astype(np.uint16)


def unstriped(offs):
    return offs[:16].T.reshape(-1).astype(np.int64)


E2M1 = np.array([0.0, 0.5, 1.0, 1.5, 2.0, 3.0, 4.0, 6.0, -0.0, -0.5, -1.0, -1.5, -2.0, -3.0, -4.0, -6.0])


def pack_weight(w, fmt):
    k, n = w.shape
    w = f64(np.asarray(w, np.float32).astype(ml_dtypes.bfloat16)).reshape(k // 32, 32, n)
    amax = np.abs(w).max(1)
    if fmt == "e4m3":
        byte = np.frexp(amax)[1] - 1 + 127 - 7
    else:
        mant, ex = np.frexp(amax / 6.0)
        byte = np.where(mant > 0.5, ex, ex - 1) + 127
    byte = np.clip(np.where(amax > 0, byte, 1), 1, 254)
    scaled = (w * np.exp2(127.0 - byte)[:, None, :]).reshape(k, n).astype(np.float32)
    by_word = np.ascontiguousarray(scaled.reshape(k // 512, 128, 4, n).transpose(0, 1, 3, 2))
    if fmt == "e4m3":
        words = by_word.astype(ml_dtypes.float8_e4m3fn).view(np.uint8)
    else:
        c = by_word.astype(ml_dtypes.float4_e2m1fn).view(np.uint8) & 0xF
        words = (c[..., 0::2] | (c[..., 1::2] << 4)).reshape(k // 512, 128, 2 * n)
    return np.ascontiguousarray(words), np.ascontiguousarray(byte.astype(np.uint8).reshape(k // 512, 16, n))


def unpack_weight(words, scales, fmt):
    g, _, n = scales.shape
    words = np.ascontiguousarray(words).reshape(g, 128, n, -1)
    if fmt == "e4m3":
        vals = words.view(ml_dtypes.float8_e4m3fn).astype(np.float64)
    else:
        nib = np.empty((g, 128, n, 4), np.uint8)
        nib[..., 0::2] = words & 0xF
        nib[..., 1::2] = words >> 4
        vals = E2M1[nib]
    vals = vals * np.repeat(np.exp2(scales.astype(np.float64) - 127.0), 8, axis=1)[..., None]
    return vals.transpose(0, 1, 3, 2).reshape(g * 512, n)


def bf(x):
    return np.asarray(x, np.float32).astype(ml_dtypes.bfloat16)


def planes(Y):
    r, m = Y.shape
    b = f64(bf(Y)).reshape(r // 32, 32, m)
    amax = np.abs(b).max(1)
    byte = np.clip(np.where(amax > 0, np.frexp(amax)[1] - 1 + 127 - 7, 1), 1, 254)
    codes = (b * np.exp2(127.0 - byte)[:, None, :]).reshape(r, m).astype(np.float32).astype(ml_dtypes.float8_e4m3fn).view(np.uint8)
    words = codes.reshape(r // 512, 128, 4, m).transpose(0, 1, 3, 2)
    return np.ascontiguousarray(words), np.ascontiguousarray(byte.astype(np.uint8).reshape(r // 512, 16, m))


D, T, I, J, U, Z, M, N = 512, 2048, 512, 512, 1024, 1024, 512, 64


def setup_inputs():
    n = np.random.standard_normal
    idx = np.random.permutation(T)[:I]
    idx2 = np.random.permutation(U)[:J]
    idx3 = np.random.permutation(Z)[:J]
    idx4 = np.random.permutation(M)[:N]
    fd = mx_kscale(D)
    keysp = pack_weight(n((D, T)) / fd[:, None], "e2m1")
    return {
        "keys_words": keysp[0],
        "keys_scales": keysp[1],
        "notes": (n((D, U)) * 1.0 / np.sqrt(D) * fd[:, None]).astype(np.float32),
        "users2": (n((D, Z)) * 1.0 / np.sqrt(D) * fd[:, None]).astype(np.float32),
        "old": (1.0 * n((I, M))).astype(np.float32),
        "offs": striped(idx),
        "offs2": striped(idx2),
        "offs3": striped(idx3),
        "offs4": striped(idx4),
    }


def reference(keys_words, keys_scales, notes, users2, old, offs, offs2, offs3, offs4):
    idx = unstriped(offs)
    idx2 = unstriped(offs2)
    idx3 = unstriped(offs3)
    idx4 = unstriped(offs4)
    keysu = unpack_weight(keys_words, keys_scales, "e2m1")
    keysidxg = keysu[:, idx]
    notesidx2q = mxq(f64(notes)[:, idx2], 0, "e4m3")
    g1 = keysidxg.T @ notesidx2q
    users2idx3q = mxq(f64(users2)[:, idx3], 0, "e4m3")
    g2 = keysidxg.T @ users2idx3q
    g0 = np.maximum(g1, g2)
    rb0 = g0.reshape(I, N, J // N).max(axis=2)
    gf = np.zeros((I, M))
    gf[:, idx4] = rb0
    y = f64(old) + gf
    words, scales = planes(y)
    return y, words, scales

@@ -1,0 +1,164 @@
+from contextlib import ExitStack
+
+import concourse.mybir as mybir
+
+D, T, I, J, U, M, N = 512, 2048, 512, 512, 1024, 512, 64
+FLOPS = 2 * 2 * D * I * J
+
+F32 = mybir.dt.float32
+BF16 = mybir.dt.bfloat16
+I32 = mybir.dt.int32
+U32 = mybir.dt.uint32
+U16 = mybir.dt.uint16
+U8 = mybir.dt.uint8
+FP8X4 = mybir.dt.float8_e4m3fn_x4
+FP4X4 = mybir.dt.float4_e2m1fn_x4
+COPY = mybir.ActivationFunctionType.Copy
+MAX = mybir.AluOpType.max
+ADD = mybir.AluOpType.add
+AXIS_X = mybir.AxisListType.X
+
+P = 128
+PACK = 4
+RUN = J // N
+HALF = M // 2
+NOTE_VECTOR_SHARE = (0, 384, 0, 384)
+USER_VECTOR_SHARE = (256, 0, 0, 384)
+
+
+def tile_attend_tab_larger_runsput_pl_kernel(
+    tc, keys_words, keys_scales, notes, users2, old, offs, offs2, offs3, offs4, out_0, out_1, out_2
+):
+    nc = tc.nc
+    with ExitStack() as ctx:
+        keep = ctx.enter_context(tc.tile_pool(name="keep", bufs=1))
+        psum = ctx.enter_context(tc.psum_pool(name="psum", bufs=1))
+
+        key_list = keep.tile([P, I // 16], U16, name="key_list")
+        note_list = keep.tile([P, J // 16], U16, name="note_list")
+        user_list = keep.tile([P, J // 16], U16, name="user_list")
+        put_list = keep.tile([P, N // 16], U16, name="put_list")
+        pool_words = keep.tile([P, T], U16, name="pool_words", align_bytes=64)
+        pool_scales = keep.tile([P, T], U8, name="pool_scales", align_bytes=64)
+        note_planes = [keep.tile([P, U], F32, name="note_plane%d" % t) for t in range(PACK)]
+        user_planes = [keep.tile([P, U], F32, name="user_plane%d" % t) for t in range(PACK)]
+        old_rows = keep.tile([P, PACK, M], F32, name="old_rows")
+        put = [keep.tile([P, M], F32, name="put%d" % t) for t in range(PACK)]
+
+        nc.vector.memset(pool_scales[:].bitcast(I32), 0)
+        for q in range(4):
+            nc.scalar.dma_start(
+                out=pool_scales[32 * q : 32 * q + 4, :].bitcast(I32),
+                in_=keys_scales[0, 4 * q : 4 * q + 4, :].bitcast(I32),
+            )
+        notes_v = notes.rearrange("(p t) u -> p t u", t=PACK)
+        users_v = users2.rearrange("(p t) u -> p t u", t=PACK)
+        nc.sync.dma_start(key_list[:], offs)
+        nc.sync.dma_start(out=pool_words[:].bitcast(I32), in_=keys_words[0].bitcast(I32))
+        nc.sync.dma_start(note_list[:], offs2)
+        for t in range(PACK):
+            nc.sync.dma_start(out=note_planes[t][:], in_=notes_v[:, t, :])
+        nc.sync.dma_start(user_list[:], offs3)
+        for t in range(PACK):
+            nc.sync.dma_start(out=user_planes[t][:], in_=users_v[:, t, :])
+        nc.sync.dma_start(put_list[:], offs4)
+        nc.sync.dma_start(out=old_rows[:], in_=old.rearrange("(p t) m -> p t m", t=PACK))
+        for t in range(PACK):
+            nc.vector.memset(put[t][:], 0.0)
+
+        got_words = keep.tile([P, I], U16, name="got_words", align_bytes=64)
+        key_words = keep.tile([P, I], U16, name="key_words", align_bytes=64)
+        key_scales = keep.tile([P, I], U8, name="key_scales", align_bytes=64)
+        nc.vector.tensor_copy(got_words[:], pool_words[:].indirect(key_list[:]))
+        nc.vector.tensor_copy(
+            key_words[:].rearrange("p (t s) -> p t s", t=PACK), got_words[:].rearrange("p (s t) -> p t s", t=PACK)
+        )
+        nc.vector.tensor_copy(
+            key_scales[:].rearrange("p (t s) -> p s t", t=PACK), pool_scales[:].indirect(key_list[:])
+        )
+
+        def products(name, planes, picks, vector_share):
+            got = keep.tile([P, PACK, J], BF16, name=name + "_got", align_bytes=64)
+            woven = keep.tile([P, J, PACK], BF16, name=name + "_woven", align_bytes=64)
+            codes = keep.tile([P, J], U32, name=name + "_codes", align_bytes=64)
+            scales = keep.tile([P, J], U8, name=name + "_scales", align_bytes=64)
+            for t in range(PACK):
+                cut = vector_share[t]
+                if cut > 0:
+                    nc.vector.tensor_copy(got[:, t, 0:cut], planes[t][:].indirect(picks[:, 0 : cut // 16]))
+                nc.scalar.activation(got[:, t, cut:J], planes[t][:].indirect(picks[:, cut // 16 : J // 16]), COPY)
+                if t % 2 == 1:
+                    pair = slice(t - 1, t + 1)
+                    nc.vector.tensor_copy(woven[:, :, pair], got[:, pair, :].rearrange("p t j -> p j t"))
+            nc.vector.quantize_mx(
+                out=codes[:].bitcast(FP8X4), scales=scales[:], in_=woven[:].rearrange("p j t -> p (j t)")
+            )
+            banks = []
+            for t in range(PACK):
+                bank = psum.tile([P, J], F32, name=name + "_bank%d" % t)
+                cols = slice(t * P, (t + 1) * P)
+                nc.tensor.matmul_mx(
+                    out=bank[:],
+                    lhsT=key_words[:, cols].bitcast(FP4X4),
+                    lhsT_scale=key_scales[:, cols],
+                    rhs=codes[:].bitcast(FP8X4),
+                    rhs_scale=scales[:],
+                    start=True,
+                    stop=True,
+                )
+                banks.append(bank)
+            return banks
+
+        def run_max(dst, bank):
+            nc.vector.tensor_reduce(dst, bank[:].rearrange("p (n r) -> p n r", r=RUN), AXIS_X, MAX)
+
+        user_max = [keep.tile([P, N], F32, name="user_max%d" % t) for t in range(PACK)]
+        both_max = [keep.tile([P, N], F32, name="both_max%d" % t) for t in range(PACK)]
+        y_low = keep.tile([P, 2, M], F32, name="y_low")
+        y_high = [keep.tile([P, 2, HALF], F32, name="y_high%d" % h) for h in range(2)]
+        y_woven = [keep.tile([P, HALF, PACK], BF16, name="y_woven%d" % h, align_bytes=64) for h in range(2)]
+        y_codes = [keep.tile([P, HALF], U32, name="y_codes%d" % h, align_bytes=64) for h in range(2)]
+        y_scales = keep.tile([P, M], U8, name="y_scales", align_bytes=64)
+        out_rows = out_0.rearrange("(p t) m -> p t m", t=PACK)
+        out_words = out_1[0].rearrange("p c r -> p (c r)").bitcast(I32)
+        halves = [slice(h * HALF, (h + 1) * HALF) for h in range(2)]
+
+        note_banks = products("note", note_planes, note_list, NOTE_VECTOR_SHARE)
+        note_max = [keep.tile([P, N], F32, name="note_max%d" % t) for t in range(PACK - 1)]
+        for t in range(PACK - 1):
+            run_max(note_max[t][:], note_banks[t])
+        user_banks = products("user", user_planes, user_list, USER_VECTOR_SHARE)
+        note_max.append(keep.tile([P, N], F32, name="note_max_last", tag="user_woven", align_bytes=64))
+        run_max(note_max[PACK - 1][:], note_banks[PACK - 1])
+
+        def add_old(t):
+            if t < 2:
+                nc.vector.tensor_tensor(y_low[:, t, :], old_rows[:, t, :], put[t][:], ADD)
+                nc.sync.dma_start(out=out_rows[:, t, :], in_=y_low[:, t, :])
+            else:
+                for h in range(2):
+                    nc.vector.tensor_tensor(y_high[h][:, t - 2, :], old_rows[:, t, halves[h]], put[t][:, halves[h]], ADD)
+
+        for t in range(PACK):
+            run_max(user_max[t][:], user_banks[t])
+            nc.vector.tensor_tensor(both_max[t][:], note_max[t][:], user_max[t][:], MAX)
+            nc.scalar.activation(put[t][:].indirect(put_list[:]), both_max[t][:], COPY)
+        for t in range(PACK):
+            add_old(t)
+        for h in range(2):
+            nc.sync.dma_start(out=out_rows[:, 2:4, halves[h]], in_=y_high[h][:])
+            nc.scalar.copy(y_woven[h][:, :, 0:2], y_low[:, :, halves[h]].rearrange("p t m -> p m t"))
+        for h in range(2):
+            nc.vector.tensor_copy(y_woven[h][:, :, 2:4], y_high[h][:].rearrange("p t m -> p m t"))
+        for h in range(2):
+            nc.vector.quantize_mx(
+                out=y_codes[h][:].bitcast(FP8X4),
+                scales=y_scales[:, halves[h]],
+                in_=y_woven[h][:].rearrange("p m t -> p (m t)"),
+            )
+            nc.sync.dma_start(out=out_words[:, halves[h]], in_=y_codes[h][:].bitcast(I32))
+        for q in range(4):
+            queue = nc.scalar if q % 2 == 0 else nc.sync
+            queue.dma_start(
+                out=out_2[0, 4 * q : 4 * q + 4, :].bitcast(I32), in_=y_scales[32 * q : 32 * q + 4, :].bitcast(I32)
+            )

@@ -22,8 +22,8 @@ P = 128
 PACK = 4
 RUN = J // N
 HALF = M // 2
-NOTE_VECTOR_SHARE = (0, 384, 0, 384)
-USER_VECTOR_SHARE = (256, 0, 0, 384)
+NOTE_VECTOR_SHARE = (0, 256, 256, 256)
+USER_VECTOR_SHARE = (256, 0, 0, 256)
 
 
 def tile_attend_tab_larger_runsput_pl_kernel(
@@ -41,7 +41,7 @@ def tile_attend_tab_larger_runsput_pl_kernel(
         pool_words = keep.tile([P, T], U16, name="pool_words", align_bytes=64)
         pool_scales = keep.tile([P, T], U8, name="pool_scales", align_bytes=64)
         note_planes = [keep.tile([P, U], F32, name="note_plane%d" % t) for t in range(PACK)]
-        user_planes = [keep.tile([P, U], F32, name="user_plane%d" % t) for t in range(PACK)]
+        user_planes = [keep.tile([P, U], F32, name="user_plane%d" % t, align_bytes=64) for t in range(PACK)]
         old_rows = keep.tile([P, PACK, M], F32, name="old_rows")
         put = [keep.tile([P, M], F32, name="put%d" % t) for t in range(PACK)]
 
@@ -77,35 +77,38 @@ def tile_attend_tab_larger_runsput_pl_kernel(
             key_scales[:].rearrange("p (t s) -> p s t", t=PACK), pool_scales[:].indirect(key_list[:])
         )
 
-        def products(name, planes, picks, vector_share):
+        halves = [slice(h * HALF, (h + 1) * HALF) for h in range(2)]
+
+        def products(name, planes, picks, vector_share, second_weave):
             got = keep.tile([P, PACK, J], BF16, name=name + "_got", align_bytes=64)
-            woven = keep.tile([P, J, PACK], BF16, name=name + "_woven", align_bytes=64)
-            codes = keep.tile([P, J], U32, name=name + "_codes", align_bytes=64)
-            scales = keep.tile([P, J], U8, name=name + "_scales", align_bytes=64)
+            woven = [keep.tile([P, HALF, PACK], BF16, name=name + "_woven%d" % h, align_bytes=64) for h in range(2)]
+            codes = [keep.tile([P, HALF], U32, name=name + "_codes%d" % h, align_bytes=64) for h in range(2)]
+            scales = [keep.tile([P, HALF], U8, name=name + "_scales%d" % h, align_bytes=64) for h in range(2)]
             for t in range(PACK):
                 cut = vector_share[t]
                 if cut > 0:
                     nc.vector.tensor_copy(got[:, t, 0:cut], planes[t][:].indirect(picks[:, 0 : cut // 16]))
                 nc.scalar.activation(got[:, t, cut:J], planes[t][:].indirect(picks[:, cut // 16 : J // 16]), COPY)
-                if t % 2 == 1:
-                    pair = slice(t - 1, t + 1)
-                    nc.vector.tensor_copy(woven[:, :, pair], got[:, pair, :].rearrange("p t j -> p j t"))
-            nc.vector.quantize_mx(
-                out=codes[:].bitcast(FP8X4), scales=scales[:], in_=woven[:].rearrange("p j t -> p (j t)")
-            )
+            for h, weave in enumerate((nc.vector.tensor_copy, second_weave)):
+                weave(woven[h][:], got[:, :, halves[h]].rearrange("p t j -> p j t"))
+            for h in range(2):
+                nc.vector.quantize_mx(
+                    out=codes[h][:].bitcast(FP8X4), scales=scales[h][:], in_=woven[h][:].rearrange("p j t -> p (j t)")
+                )
             banks = []
             for t in range(PACK):
                 bank = psum.tile([P, J], F32, name=name + "_bank%d" % t)
                 cols = slice(t * P, (t + 1) * P)
-                nc.tensor.matmul_mx(
-                    out=bank[:],
-                    lhsT=key_words[:, cols].bitcast(FP4X4),
-                    lhsT_scale=key_scales[:, cols],
-                    rhs=codes[:].bitcast(FP8X4),
-                    rhs_scale=scales[:],
-                    start=True,
-                    stop=True,
-                )
+                for h in range(2):
+                    nc.tensor.matmul_mx(
+                        out=bank[:, halves[h]],
+                        lhsT=key_words[:, cols].bitcast(FP4X4),
+                        lhsT_scale=key_scales[:, cols],
+                        rhs=codes[h][:].bitcast(FP8X4),
+                        rhs_scale=scales[h][:],
+                        start=True,
+                        stop=True,
+                    )
                 banks.append(bank)
             return banks
 
@@ -114,42 +117,43 @@ def tile_attend_tab_larger_runsput_pl_kernel(
 
         user_max = [keep.tile([P, N], F32, name="user_max%d" % t) for t in range(PACK)]
         both_max = [keep.tile([P, N], F32, name="both_max%d" % t) for t in range(PACK)]
-        y_low = keep.tile([P, 2, M], F32, name="y_low")
-        y_high = [keep.tile([P, 2, HALF], F32, name="y_high%d" % h) for h in range(2)]
+        y = [keep.tile([P, PACK, HALF], F32, name="y%d" % h) for h in range(2)]
         y_woven = [keep.tile([P, HALF, PACK], BF16, name="y_woven%d" % h, align_bytes=64) for h in range(2)]
         y_codes = [keep.tile([P, HALF], U32, name="y_codes%d" % h, align_bytes=64) for h in range(2)]
         y_scales = keep.tile([P, M], U8, name="y_scales", align_bytes=64)
         out_rows = out_0.rearrange("(p t) m -> p t m", t=PACK)
         out_words = out_1[0].rearrange("p c r -> p (c r)").bitcast(I32)
-        halves = [slice(h * HALF, (h + 1) * HALF) for h in range(2)]
 
-        note_banks = products("note", note_planes, note_list, NOTE_VECTOR_SHARE)
-        note_max = [keep.tile([P, N], F32, name="note_max%d" % t) for t in range(PACK - 1)]
-        for t in range(PACK - 1):
+        note_banks = products("note", note_planes, note_list, NOTE_VECTOR_SHARE, nc.vector.tensor_copy)
+        note_max = [keep.tile([P, N], F32, name="note_max%d" % t) for t in range(2)]
+        for t in range(2):
             run_max(note_max[t][:], note_banks[t])
-        user_banks = products("user", user_planes, user_list, USER_VECTOR_SHARE)
-        note_max.append(keep.tile([P, N], F32, name="note_max_last", tag="user_woven", align_bytes=64))
-        run_max(note_max[PACK - 1][:], note_banks[PACK - 1])
+        user_banks = products("user", user_planes, user_list, USER_VECTOR_SHARE, nc.scalar.copy)
+        for t, tag in ((2, "user_plane3"), (3, "user_woven1")):
+            note_max.append(keep.tile([P, N], F32, name="note_max%d" % t, tag=tag, align_bytes=64))
+            run_max(note_max[t][:], note_banks[t])
+
+        def put_max(t):
+            nc.vector.tensor_tensor(both_max[t][:], note_max[t][:], user_max[t][:], MAX)
+            nc.scalar.activation(put[t][:].indirect(put_list[:]), both_max[t][:], COPY)
 
         def add_old(t):
-            if t < 2:
-                nc.vector.tensor_tensor(y_low[:, t, :], old_rows[:, t, :], put[t][:], ADD)
-                nc.sync.dma_start(out=out_rows[:, t, :], in_=y_low[:, t, :])
-            else:
-                for h in range(2):
-                    nc.vector.tensor_tensor(y_high[h][:, t - 2, :], old_rows[:, t, halves[h]], put[t][:, halves[h]], ADD)
+            for h in range(2):
+                nc.vector.tensor_tensor(y[h][:, t, :], old_rows[:, t, halves[h]], put[t][:, halves[h]], ADD)
+                if t % 2 == 1:
+                    pair = slice(t - 1, t + 1)
+                    nc.sync.dma_start(out=out_rows[:, pair, halves[h]], in_=y[h][:, pair, :])
 
         for t in range(PACK):
             run_max(user_max[t][:], user_banks[t])
-            nc.vector.tensor_tensor(both_max[t][:], note_max[t][:], user_max[t][:], MAX)
-            nc.scalar.activation(put[t][:].indirect(put_list[:]), both_max[t][:], COPY)
-        for t in range(PACK):
+            if t > 0:
+                put_max(t - 1)
+        add_old(0)
+        put_max(PACK - 1)
+        for t in range(1, PACK):
             add_old(t)
-        for h in range(2):
-            nc.sync.dma_start(out=out_rows[:, 2:4, halves[h]], in_=y_high[h][:])
-            nc.scalar.copy(y_woven[h][:, :, 0:2], y_low[:, :, halves[h]].rearrange("p t m -> p m t"))
-        for h in range(2):
-            nc.vector.tensor_copy(y_woven[h][:, :, 2:4], y_high[h][:].rearrange("p t m -> p m t"))
+        nc.scalar.copy(y_woven[0][:], y[0][:].rearrange("p t m -> p m t"))
+        nc.vector.tensor_copy(y_woven[1][:], y[1][:].rearrange("p t m -> p m t"))
         for h in range(2):
             nc.vector.quantize_mx(
                 out=y_codes[h][:].bitcast(FP8X4),

@@ -23,6 +23,7 @@ PACK = 4
 RUN = J // N
 HALF = M // 2
 NOTE_VECTOR_SHARE = (0, 256, 256, 256)
+Y_VECTOR_HEAD = 128
 USER_VECTOR_SHARE = (256, 0, 0, 256)
 
 
@@ -79,44 +80,43 @@ def tile_attend_tab_larger_runsput_pl_kernel(
 
         halves = [slice(h * HALF, (h + 1) * HALF) for h in range(2)]
 
-        def products(name, planes, picks, vector_share, second_weave):
+        def weave(copy, dst, src):
+            copy(dst.rearrange("p (c i) t -> p c t i", i=4), src.rearrange("p t (c i) -> p c t i", i=4))
+
+        def gather_planes(name, planes, picks, vector_share):
             got = keep.tile([P, PACK, J], BF16, name=name + "_got", align_bytes=64)
-            woven = [keep.tile([P, HALF, PACK], BF16, name=name + "_woven%d" % h, align_bytes=64) for h in range(2)]
-            codes = [keep.tile([P, HALF], U32, name=name + "_codes%d" % h, align_bytes=64) for h in range(2)]
-            scales = [keep.tile([P, HALF], U8, name=name + "_scales%d" % h, align_bytes=64) for h in range(2)]
             for t in range(PACK):
                 cut = vector_share[t]
                 if cut > 0:
                     nc.vector.tensor_copy(got[:, t, 0:cut], planes[t][:].indirect(picks[:, 0 : cut // 16]))
                 nc.scalar.activation(got[:, t, cut:J], planes[t][:].indirect(picks[:, cut // 16 : J // 16]), COPY)
-            for h, weave in enumerate((nc.vector.tensor_copy, second_weave)):
-                weave(woven[h][:], got[:, :, halves[h]].rearrange("p t j -> p j t"))
-            for h in range(2):
-                nc.vector.quantize_mx(
-                    out=codes[h][:].bitcast(FP8X4), scales=scales[h][:], in_=woven[h][:].rearrange("p j t -> p (j t)")
-                )
-            banks = []
-            for t in range(PACK):
-                bank = psum.tile([P, J], F32, name=name + "_bank%d" % t)
-                cols = slice(t * P, (t + 1) * P)
-                for h in range(2):
-                    nc.tensor.matmul_mx(
-                        out=bank[:, halves[h]],
-                        lhsT=key_words[:, cols].bitcast(FP4X4),
-                        lhsT_scale=key_scales[:, cols],
-                        rhs=codes[h][:].bitcast(FP8X4),
-                        rhs_scale=scales[h][:],
-                        start=True,
-                        stop=True,
-                    )
-                banks.append(bank)
-            return banks
+            return got
 
-        def run_max(dst, bank):
-            nc.vector.tensor_reduce(dst, bank[:].rearrange("p (n r) -> p n r", r=RUN), AXIS_X, MAX)
+        def quantize(name, woven, width):
+            codes = keep.tile([P, width], U32, name=name + "_codes", align_bytes=64)
+            scales = keep.tile([P, width], U8, name=name + "_scales", align_bytes=64)
+            nc.vector.quantize_mx(
+                out=codes[:].bitcast(FP8X4), scales=scales[:], in_=woven[:].rearrange("p j t -> p (j t)")
+            )
+            return codes, scales
 
-        user_max = [keep.tile([P, N], F32, name="user_max%d" % t) for t in range(PACK)]
-        both_max = [keep.tile([P, N], F32, name="both_max%d" % t) for t in range(PACK)]
+        def product(dst, t, operand):
+            cols = slice(t * P, (t + 1) * P)
+            nc.tensor.matmul_mx(
+                out=dst,
+                lhsT=key_words[:, cols].bitcast(FP4X4),
+                lhsT_scale=key_scales[:, cols],
+                rhs=operand[0][:].bitcast(FP8X4),
+                rhs_scale=operand[1][:],
+                start=True,
+                stop=True,
+            )
+
+        def run_max(name, bank, tag):
+            runs = keep.tile([P, N], F32, name=name, tag=tag, align_bytes=64)
+            nc.vector.tensor_reduce(runs[:], bank[:].rearrange("p (n r) -> p n r", r=RUN), AXIS_X, MAX)
+            return runs
+
         y = [keep.tile([P, PACK, HALF], F32, name="y%d" % h) for h in range(2)]
         y_woven = [keep.tile([P, HALF, PACK], BF16, name="y_woven%d" % h, align_bytes=64) for h in range(2)]
         y_codes = [keep.tile([P, HALF], U32, name="y_codes%d" % h, align_bytes=64) for h in range(2)]
@@ -124,36 +124,63 @@ def tile_attend_tab_larger_runsput_pl_kernel(
         out_rows = out_0.rearrange("(p t) m -> p t m", t=PACK)
         out_words = out_1[0].rearrange("p c r -> p (c r)").bitcast(I32)
 
-        note_banks = products("note", note_planes, note_list, NOTE_VECTOR_SHARE, nc.vector.tensor_copy)
-        note_max = [keep.tile([P, N], F32, name="note_max%d" % t) for t in range(2)]
-        for t in range(2):
-            run_max(note_max[t][:], note_banks[t])
-        user_banks = products("user", user_planes, user_list, USER_VECTOR_SHARE, nc.scalar.copy)
-        for t, tag in ((2, "user_plane3"), (3, "user_woven1")):
-            note_max.append(keep.tile([P, N], F32, name="note_max%d" % t, tag=tag, align_bytes=64))
-            run_max(note_max[t][:], note_banks[t])
+        note_got = gather_planes("note", note_planes, note_list, NOTE_VECTOR_SHARE)
+        note_woven = [keep.tile([P, HALF, PACK], BF16, name="note_woven%d" % h, align_bytes=64) for h in range(2)]
+        for h in range(2):
+            weave(nc.vector.tensor_copy, note_woven[h][:], note_got[:, :, halves[h]])
+        note_mx = [quantize("note%d" % h, note_woven[h], HALF) for h in range(2)]
+        early_banks = [psum.tile([P, 2, HALF], F32, name="early_bank%d" % h) for h in range(2)]
+        late_banks = [psum.tile([P, J], F32, name="late_bank%d" % e) for e in range(2)]
+        early_max = keep.tile([P, 2, N], F32, name="early_max")
+        for h in range(2):
+            for e in range(2):
+                product(early_banks[h][:, e, :], e, note_mx[h])
+            nc.vector.tensor_reduce(
+                early_max[:, :, h * N // 2 : (h + 1) * N // 2],
+                early_banks[h][:].rearrange("p e (n r) -> p e n r", r=RUN),
+                AXIS_X,
+                MAX,
+            )
+        for e in range(2):
+            for h in range(2):
+                product(late_banks[e][:, halves[h]], 2 + e, note_mx[h])
+        note_max = [early_max[:, e, :] for e in range(2)]
+
+        user_got = gather_planes("user", user_planes, user_list, USER_VECTOR_SHARE)
+        user_woven = keep.tile([P, J, PACK], BF16, name="user_woven", align_bytes=64)
+        for h, copy in enumerate((nc.vector.tensor_copy, nc.scalar.copy)):
+            weave(copy, user_woven[:, halves[h], :], user_got[:, :, halves[h]])
+        user_mx = quantize("user", user_woven, J)
+        user_banks = []
+        for t in range(PACK):
+            user_banks.append(psum.tile([P, J], F32, name="user_bank%d" % t))
+            product(user_banks[t][:], t, user_mx)
+        for e, tag in enumerate(("user_plane3", "user_woven")):
+            note_max.append(run_max("late_max%d" % e, late_banks[e], tag)[:])
+        user_max = []
 
         def put_max(t):
-            nc.vector.tensor_tensor(both_max[t][:], note_max[t][:], user_max[t][:], MAX)
-            nc.scalar.activation(put[t][:].indirect(put_list[:]), both_max[t][:], COPY)
+            both_max = keep.tile([P, N], F32, name="both_max%d" % t)
+            nc.vector.tensor_tensor(both_max[:], note_max[t], user_max[t][:], MAX)
+            nc.scalar.activation(put[t][:].indirect(put_list[:]), both_max[:], COPY)
 
-        def add_old(t):
-            for h in range(2):
-                nc.vector.tensor_tensor(y[h][:, t, :], old_rows[:, t, halves[h]], put[t][:, halves[h]], ADD)
-                if t % 2 == 1:
-                    pair = slice(t - 1, t + 1)
-                    nc.sync.dma_start(out=out_rows[:, pair, halves[h]], in_=y[h][:, pair, :])
+        def add_old(h, t):
+            nc.vector.tensor_tensor(y[h][:, t, :], old_rows[:, t, halves[h]], put[t][:, halves[h]], ADD)
+            if t % 2 == 1:
+                pair = slice(t - 1, t + 1)
+                nc.sync.dma_start(out=out_rows[:, pair, halves[h]], in_=y[h][:, pair, :])
 
         for t in range(PACK):
-            run_max(user_max[t][:], user_banks[t])
+            user_max.append(run_max("user_max%d" % t, user_banks[t], "user_max%d" % t))
             if t > 0:
                 put_max(t - 1)
-        add_old(0)
+        add_old(0, 0)
         put_max(PACK - 1)
-        for t in range(1, PACK):
-            add_old(t)
-        nc.scalar.copy(y_woven[0][:], y[0][:].rearrange("p t m -> p m t"))
-        nc.vector.tensor_copy(y_woven[1][:], y[1][:].rearrange("p t m -> p m t"))
+        for h, t in ((0, 1), (0, 2), (1, 0), (0, 3), (1, 1), (1, 2), (1, 3)):
+            add_old(h, t)
+        weave(nc.scalar.copy, y_woven[0][:], y[0][:])
+        weave(nc.vector.tensor_copy, y_woven[1][:, 0:Y_VECTOR_HEAD, :], y[1][:, :, 0:Y_VECTOR_HEAD])
+        weave(nc.scalar.copy, y_woven[1][:, Y_VECTOR_HEAD:HALF, :], y[1][:, :, Y_VECTOR_HEAD:HALF])
         for h in range(2):
             nc.vector.quantize_mx(
                 out=y_codes[h][:].bitcast(FP8X4),

@@ -24,7 +24,7 @@ RUN = J // N
 HALF = M // 2
 NOTE_VECTOR_SHARE = (0, 256, 256, 256)
 Y_VECTOR_HEAD = 128
-USER_VECTOR_SHARE = (256, 0, 0, 256)
+USER_VECTOR_SHARE = (256, 0, 0, 320)
 
 
 def tile_attend_tab_larger_runsput_pl_kernel(
@@ -92,22 +92,26 @@ def tile_attend_tab_larger_runsput_pl_kernel(
                 nc.scalar.activation(got[:, t, cut:J], planes[t][:].indirect(picks[:, cut // 16 : J // 16]), COPY)
             return got
 
-        def quantize(name, woven, width):
-            codes = keep.tile([P, width], U32, name=name + "_codes", align_bytes=64)
-            scales = keep.tile([P, width], U8, name=name + "_scales", align_bytes=64)
-            nc.vector.quantize_mx(
-                out=codes[:].bitcast(FP8X4), scales=scales[:], in_=woven[:].rearrange("p j t -> p (j t)")
-            )
+        def mx_tiles(name):
+            codes = keep.tile([P, J], U32, name=name + "_codes", align_bytes=64)
+            scales = keep.tile([P, J], U8, name=name + "_scales", align_bytes=64)
             return codes, scales
 
-        def product(dst, t, operand):
-            cols = slice(t * P, (t + 1) * P)
+        def quantize(operand, cols, woven):
+            nc.vector.quantize_mx(
+                out=operand[0][:, cols].bitcast(FP8X4),
+                scales=operand[1][:, cols],
+                in_=woven[:].rearrange("p j t -> p (j t)"),
+            )
+
+        def product(dst, t, operand, cols):
+            rows = slice(t * P, (t + 1) * P)
             nc.tensor.matmul_mx(
                 out=dst,
-                lhsT=key_words[:, cols].bitcast(FP4X4),
-                lhsT_scale=key_scales[:, cols],
-                rhs=operand[0][:].bitcast(FP8X4),
-                rhs_scale=operand[1][:],
+                lhsT=key_words[:, rows].bitcast(FP4X4),
+                lhsT_scale=key_scales[:, rows],
+                rhs=operand[0][:, cols].bitcast(FP8X4),
+                rhs_scale=operand[1][:, cols],
                 start=True,
                 stop=True,
             )
@@ -128,13 +132,15 @@ def tile_attend_tab_larger_runsput_pl_kernel(
         note_woven = [keep.tile([P, HALF, PACK], BF16, name="note_woven%d" % h, align_bytes=64) for h in range(2)]
         for h in range(2):
             weave(nc.vector.tensor_copy, note_woven[h][:], note_got[:, :, halves[h]])
-        note_mx = [quantize("note%d" % h, note_woven[h], HALF) for h in range(2)]
+        note_mx = mx_tiles("note")
+        for h in range(2):
+            quantize(note_mx, halves[h], note_woven[h])
         early_banks = [psum.tile([P, 2, HALF], F32, name="early_bank%d" % h) for h in range(2)]
         late_banks = [psum.tile([P, J], F32, name="late_bank%d" % e) for e in range(2)]
         early_max = keep.tile([P, 2, N], F32, name="early_max")
         for h in range(2):
             for e in range(2):
-                product(early_banks[h][:, e, :], e, note_mx[h])
+                product(early_banks[h][:, e, :], e, note_mx, halves[h])
             nc.vector.tensor_reduce(
                 early_max[:, :, h * N // 2 : (h + 1) * N // 2],
                 early_banks[h][:].rearrange("p e (n r) -> p e n r", r=RUN),
@@ -142,19 +148,19 @@ def tile_attend_tab_larger_runsput_pl_kernel(
                 MAX,
             )
         for e in range(2):
-            for h in range(2):
-                product(late_banks[e][:, halves[h]], 2 + e, note_mx[h])
+            product(late_banks[e][:], 2 + e, note_mx, slice(0, J))
         note_max = [early_max[:, e, :] for e in range(2)]
 
         user_got = gather_planes("user", user_planes, user_list, USER_VECTOR_SHARE)
         user_woven = keep.tile([P, J, PACK], BF16, name="user_woven", align_bytes=64)
         for h, copy in enumerate((nc.vector.tensor_copy, nc.scalar.copy)):
             weave(copy, user_woven[:, halves[h], :], user_got[:, :, halves[h]])
-        user_mx = quantize("user", user_woven, J)
+        user_mx = mx_tiles("user")
+        quantize(user_mx, slice(0, J), user_woven)
         user_banks = []
         for t in range(PACK):
             user_banks.append(psum.tile([P, J], F32, name="user_bank%d" % t))
-            product(user_banks[t][:], t, user_mx)
+            product(user_banks[t][:], t, user_mx, slice(0, J))
         for e, tag in enumerate(("user_plane3", "user_woven")):
             note_max.append(run_max("late_max%d" % e, late_banks[e], tag)[:])
         user_max = []

from contextlib import ExitStack

import concourse.mybir as mybir

D, T, I, J, U, M, N = 512, 2048, 512, 512, 1024, 512, 64
FLOPS = 2 * 2 * D * I * J

F32 = mybir.dt.float32
BF16 = mybir.dt.bfloat16
I32 = mybir.dt.int32
U32 = mybir.dt.uint32
U16 = mybir.dt.uint16
U8 = mybir.dt.uint8
FP8X4 = mybir.dt.float8_e4m3fn_x4
FP4X4 = mybir.dt.float4_e2m1fn_x4
COPY = mybir.ActivationFunctionType.Copy
MAX = mybir.AluOpType.max
ADD = mybir.AluOpType.add
AXIS_X = mybir.AxisListType.X

P = 128
PACK = 4
RUN = J // N
HALF = M // 2
NOTE_VECTOR_SHARE = (0, 256, 256, 256)
Y_VECTOR_HEAD = 128
USER_VECTOR_SHARE = (256, 0, 0, 320)


def tile_attend_tab_larger_runsput_pl_kernel(
    tc, keys_words, keys_scales, notes, users2, old, offs, offs2, offs3, offs4, out_0, out_1, out_2
):
    nc = tc.nc
    with ExitStack() as ctx:
        keep = ctx.enter_context(tc.tile_pool(name="keep", bufs=1))
        psum = ctx.enter_context(tc.psum_pool(name="psum", bufs=1))

        key_list = keep.tile([P, I // 16], U16, name="key_list")
        note_list = keep.tile([P, J // 16], U16, name="note_list")
        user_list = keep.tile([P, J // 16], U16, name="user_list")
        put_list = keep.tile([P, N // 16], U16, name="put_list")
        pool_words = keep.tile([P, T], U16, name="pool_words", align_bytes=64)
        pool_scales = keep.tile([P, T], U8, name="pool_scales", align_bytes=64)
        note_planes = [keep.tile([P, U], F32, name="note_plane%d" % t) for t in range(PACK)]
        user_planes = [keep.tile([P, U], F32, name="user_plane%d" % t, align_bytes=64) for t in range(PACK)]
        old_rows = keep.tile([P, PACK, M], F32, name="old_rows")
        put = [keep.tile([P, M], F32, name="put%d" % t) for t in range(PACK)]

        nc.vector.memset(pool_scales[:].bitcast(I32), 0)
        for q in range(4):
            nc.scalar.dma_start(
                out=pool_scales[32 * q : 32 * q + 4, :].bitcast(I32),
                in_=keys_scales[0, 4 * q : 4 * q + 4, :].bitcast(I32),
            )
        notes_v = notes.rearrange("(p t) u -> p t u", t=PACK)
        users_v = users2.rearrange("(p t) u -> p t u", t=PACK)
        nc.sync.dma_start(key_list[:], offs)
        nc.sync.dma_start(out=pool_words[:].bitcast(I32), in_=keys_words[0].bitcast(I32))
        nc.sync.dma_start(note_list[:], offs2)
        for t in range(PACK):
            nc.sync.dma_start(out=note_planes[t][:], in_=notes_v[:, t, :])
        nc.sync.dma_start(user_list[:], offs3)
        for t in range(PACK):
            nc.sync.dma_start(out=user_planes[t][:], in_=users_v[:, t, :])
        nc.sync.dma_start(put_list[:], offs4)
        nc.sync.dma_start(out=old_rows[:], in_=old.rearrange("(p t) m -> p t m", t=PACK))
        for t in range(PACK):
            nc.vector.memset(put[t][:], 0.0)

        got_words = keep.tile([P, I], U16, name="got_words", align_bytes=64)
        key_words = keep.tile([P, I], U16, name="key_words", align_bytes=64)
        key_scales = keep.tile([P, I], U8, name="key_scales", align_bytes=64)
        nc.vector.tensor_copy(got_words[:], pool_words[:].indirect(key_list[:]))
        nc.vector.tensor_copy(
            key_words[:].rearrange("p (t s) -> p t s", t=PACK), got_words[:].rearrange("p (s t) -> p t s", t=PACK)
        )
        nc.vector.tensor_copy(
            key_scales[:].rearrange("p (t s) -> p s t", t=PACK), pool_scales[:].indirect(key_list[:])
        )

        halves = [slice(h * HALF, (h + 1) * HALF) for h in range(2)]

        def weave(copy, dst, src):
            copy(dst.rearrange("p (c i) t -> p c t i", i=4), src.rearrange("p t (c i) -> p c t i", i=4))

        def gather_planes(name, planes, picks, vector_share):
            got = keep.tile([P, PACK, J], BF16, name=name + "_got", align_bytes=64)
            for t in range(PACK):
                cut = vector_share[t]
                if cut > 0:
                    nc.vector.tensor_copy(got[:, t, 0:cut], planes[t][:].indirect(picks[:, 0 : cut // 16]))
                nc.scalar.activation(got[:, t, cut:J], planes[t][:].indirect(picks[:, cut // 16 : J // 16]), COPY)
            return got

        def mx_tiles(name):
            codes = keep.tile([P, J], U32, name=name + "_codes", align_bytes=64)
            scales = keep.tile([P, J], U8, name=name + "_scales", align_bytes=64)
            return codes, scales

        def quantize(operand, cols, woven):
            nc.vector.quantize_mx(
                out=operand[0][:, cols].bitcast(FP8X4),
                scales=operand[1][:, cols],
                in_=woven[:].rearrange("p j t -> p (j t)"),
            )

        def product(dst, t, operand, cols):
            rows = slice(t * P, (t + 1) * P)
            nc.tensor.matmul_mx(
                out=dst,
                lhsT=key_words[:, rows].bitcast(FP4X4),
                lhsT_scale=key_scales[:, rows],
                rhs=operand[0][:, cols].bitcast(FP8X4),
                rhs_scale=operand[1][:, cols],
                start=True,
                stop=True,
            )

        def run_max(name, bank, tag):
            runs = keep.tile([P, N], F32, name=name, tag=tag, align_bytes=64)
            nc.vector.tensor_reduce(runs[:], bank[:].rearrange("p (n r) -> p n r", r=RUN), AXIS_X, MAX)
            return runs

        y = [keep.tile([P, PACK, HALF], F32, name="y%d" % h) for h in range(2)]
        y_woven = [keep.tile([P, HALF, PACK], BF16, name="y_woven%d" % h, align_bytes=64) for h in range(2)]
        y_codes = [keep.tile([P, HALF], U32, name="y_codes%d" % h, align_bytes=64) for h in range(2)]
        y_scales = keep.tile([P, M], U8, name="y_scales", align_bytes=64)
        out_rows = out_0.rearrange("(p t) m -> p t m", t=PACK)
        out_words = out_1[0].rearrange("p c r -> p (c r)").bitcast(I32)

        note_got = gather_planes("note", note_planes, note_list, NOTE_VECTOR_SHARE)
        note_woven = [keep.tile([P, HALF, PACK], BF16, name="note_woven%d" % h, align_bytes=64) for h in range(2)]
        for h in range(2):
            weave(nc.vector.tensor_copy, note_woven[h][:], note_got[:, :, halves[h]])
        note_mx = mx_tiles("note")
        for h in range(2):
            quantize(note_mx, halves[h], note_woven[h])
        early_banks = [psum.tile([P, 2, HALF], F32, name="early_bank%d" % h) for h in range(2)]
        late_banks = [psum.tile([P, J], F32, name="late_bank%d" % e) for e in range(2)]
        early_max = keep.tile([P, 2, N], F32, name="early_max")
        for h in range(2):
            for e in range(2):
                product(early_banks[h][:, e, :], e, note_mx, halves[h])
            nc.vector.tensor_reduce(
                early_max[:, :, h * N // 2 : (h + 1) * N // 2],
                early_banks[h][:].rearrange("p e (n r) -> p e n r", r=RUN),
                AXIS_X,
                MAX,
            )
        for e in range(2):
            product(late_banks[e][:], 2 + e, note_mx, slice(0, J))
        note_max = [early_max[:, e, :] for e in range(2)]

        user_got = gather_planes("user", user_planes, user_list, USER_VECTOR_SHARE)
        user_woven = keep.tile([P, J, PACK], BF16, name="user_woven", align_bytes=64)
        for h, copy in enumerate((nc.vector.tensor_copy, nc.scalar.copy)):
            weave(copy, user_woven[:, halves[h], :], user_got[:, :, halves[h]])
        user_mx = mx_tiles("user")
        quantize(user_mx, slice(0, J), user_woven)
        user_banks = []
        for t in range(PACK):
            user_banks.append(psum.tile([P, J], F32, name="user_bank%d" % t))
            product(user_banks[t][:], t, user_mx, slice(0, J))
        for e, tag in enumerate(("user_plane3", "user_woven")):
            note_max.append(run_max("late_max%d" % e, late_banks[e], tag)[:])
        user_max = []

        def put_max(t):
            both_max = keep.tile([P, N], F32, name="both_max%d" % t)
            nc.vector.tensor_tensor(both_max[:], note_max[t], user_max[t][:], MAX)
            nc.scalar.activation(put[t][:].indirect(put_list[:]), both_max[:], COPY)

        def add_old(h, t):
            nc.vector.tensor_tensor(y[h][:, t, :], old_rows[:, t, halves[h]], put[t][:, halves[h]], ADD)
            if t % 2 == 1:
                pair = slice(t - 1, t + 1)
                nc.sync.dma_start(out=out_rows[:, pair, halves[h]], in_=y[h][:, pair, :])

        for t in range(PACK):
            user_max.append(run_max("user_max%d" % t, user_banks[t], "user_max%d" % t))
            if t > 0:
                put_max(t - 1)
        add_old(0, 0)
        put_max(PACK - 1)
        for h, t in ((0, 1), (0, 2), (1, 0), (0, 3), (1, 1), (1, 2), (1, 3)):
            add_old(h, t)
        weave(nc.scalar.copy, y_woven[0][:], y[0][:])
        weave(nc.vector.tensor_copy, y_woven[1][:, 0:Y_VECTOR_HEAD, :], y[1][:, :, 0:Y_VECTOR_HEAD])
        weave(nc.scalar.copy, y_woven[1][:, Y_VECTOR_HEAD:HALF, :], y[1][:, :, Y_VECTOR_HEAD:HALF])
        for h in range(2):
            nc.vector.quantize_mx(
                out=y_codes[h][:].bitcast(FP8X4),
                scales=y_scales[:, halves[h]],
                in_=y_woven[h][:].rearrange("p m t -> p (m t)"),
            )
            nc.sync.dma_start(out=out_words[:, halves[h]], in_=y_codes[h][:].bitcast(I32))
        for q in range(4):
            queue = nc.scalar if q % 2 == 0 else nc.sync
            queue.dma_start(
                out=out_2[0, 4 * q : 4 * q + 4, :].bitcast(I32), in_=y_scales[32 * q : 32 * q + 4, :].bitcast(I32)
            )
